import numpy as np
import ml_dtypes

BF16 = ml_dtypes.bfloat16


def bf(x):
    return np.asarray(x, np.float32).astype(BF16)


def f32(x):
    return np.asarray(x, np.float32)


def f64(x):
    return np.asarray(x).astype(np.float64)


def striped(idx):
    return np.concatenate([l.reshape(-1, 16).T for l in idx])


def rows(idx, k):
    return np.tile(np.repeat(idx, 16, axis=0), (k // (16 * 8), 1))


def look(tab, idx):
    return np.take_along_axis(f64(tab), rows(idx, len(tab)), axis=1)


K, S, H, V, N = 128, 2048, 256, 1024, 1024


def setup_inputs():
    return {"z": bf(np.random.standard_normal((H, S))), "wt": bf(np.random.standard_normal((H, K)) / np.sqrt(H)), "base": f32(1.0 * np.random.standard_normal((K, V))), "offs": striped(np.stack([np.random.permutation(S)[:N] for _ in range(8)]))}


def reference(z, wt, base, offs):
    idx = np.stack([g.T.reshape(-1) for g in np.split(offs, 8)])
    tab = f64(wt).T @ f64(z)
    x = f64(base) + look(tab, idx)
    return x

@@ -1,0 +1,56 @@
+import concourse.mybir as mybir
+
+P = 128
+BANK = 512
+PIECE = 512
+GROUP = 16
+
+FLOPS = 2 * 256 * 128 * 2048
+
+BF16, F32, U16 = mybir.dt.bfloat16, mybir.dt.float32, mybir.dt.uint16
+
+
+def tile_lookup_pjadd_out_kernel(tc, z, wt, base, offs, out):
+    nc = tc.nc
+    features, places = z.shape
+    entries = base.shape[1]
+    passes = features // P
+
+    z_rows = z.rearrange("(p k) s -> p k s", k=passes)
+    wt_rows = wt.rearrange("(p k) r -> p k r", k=passes)
+
+    with (
+        tc.tile_pool(name="held", bufs=1) as held,
+        tc.psum_pool(name="psum", bufs=1) as psum,
+    ):
+        weights = held.tile([P, passes, P], BF16, name="weights")
+        nc.scalar.dma_start(weights[:], wt_rows)
+
+        chunks = []
+        for c in range(places // BANK):
+            chunk = held.tile([P, passes, BANK], BF16, name=f"chunk{c}")
+            nc.sync.dma_start(chunk[:], z_rows[:, :, c * BANK : (c + 1) * BANK])
+            chunks.append(chunk)
+
+        offsets = held.tile([P, entries // GROUP], U16, name="offsets")
+        nc.sync.dma_start(offsets[:], offs)
+        streams = []
+        for u in range(entries // PIECE):
+            stream = held.tile([P, PIECE], F32, name=f"stream{u}")
+            nc.sync.dma_start(stream[:], base[:, u * PIECE : (u + 1) * PIECE])
+            streams.append(stream)
+
+        table = held.tile([P, places], F32, name="table")
+        for c, chunk in enumerate(chunks):
+            bank = psum.tile([P, BANK], F32, name=f"bank{c}")
+            for k in range(passes):
+                nc.tensor.matmul(bank[:], weights[:, k, :], chunk[:, k, :], start=(k == 0), stop=(k == passes - 1))
+            copy = nc.scalar.copy if c % 2 == 0 else nc.vector.tensor_copy
+            copy(table[:, c * BANK : (c + 1) * BANK], bank[:])
+
+        columns = PIECE // GROUP
+        for u, stream in enumerate(streams):
+            summed = held.tile([P, PIECE], F32, name=f"summed{u}")
+            looked_up = table[:].indirect(offsets[:, u * columns : (u + 1) * columns])
+            nc.vector.tensor_tensor(summed[:], looked_up, stream[:], mybir.AluOpType.add)
+            nc.sync.dma_start(out[:, u * PIECE : (u + 1) * PIECE], summed[:])

@@ -1,9 +1,12 @@
 import concourse.mybir as mybir
 
 P = 128
-BANK = 512
+CHUNK = 512
+HALF = CHUNK // 2
+BANKS = 8
 PIECE = 512
 GROUP = 16
+WARM = 3
 
 FLOPS = 2 * 256 * 128 * 2048
 
@@ -21,36 +24,40 @@ def tile_lookup_pjadd_out_kernel(tc, z, wt, base, offs, out):
 
     with (
         tc.tile_pool(name="held", bufs=1) as held,
-        tc.psum_pool(name="psum", bufs=1) as psum,
+        tc.psum_pool(name="psum", bufs=BANKS) as psum,
     ):
         weights = held.tile([P, passes, P], BF16, name="weights")
         nc.scalar.dma_start(weights[:], wt_rows)
 
-        chunks = []
-        for c in range(places // BANK):
-            chunk = held.tile([P, passes, BANK], BF16, name=f"chunk{c}")
-            nc.sync.dma_start(chunk[:], z_rows[:, :, c * BANK : (c + 1) * BANK])
-            chunks.append(chunk)
+        z_tile = held.tile([P, passes, places], BF16, name="z_tile")
+        for start in range(0, places, CHUNK):
+            for k in range(passes):
+                nc.sync.dma_start(z_tile[:, k, start : start + CHUNK], z_rows[:, k, start : start + CHUNK])
 
         offsets = held.tile([P, entries // GROUP], U16, name="offsets")
         nc.sync.dma_start(offsets[:], offs)
-        streams = []
-        for u in range(entries // PIECE):
-            stream = held.tile([P, PIECE], F32, name=f"stream{u}")
-            nc.sync.dma_start(stream[:], base[:, u * PIECE : (u + 1) * PIECE])
-            streams.append(stream)
+        stream = held.tile([P, entries], F32, name="stream")
+        for start in range(0, entries, PIECE):
+            nc.sync.dma_start(stream[:, start : start + PIECE], base[:, start : start + PIECE])
+
+        zeros = held.tile([P, P], F32, name="zeros")
+        nc.vector.memset(zeros[:], 0.0)
+        unread = psum.tile([P, WARM, P], F32, name="unread", tag="bank")
+        nc.tensor.matmul(unread[:], zeros[:], zeros[:].unsqueeze(1).to_broadcast([P, WARM, P]), start=True, stop=True)
 
         table = held.tile([P, places], F32, name="table")
-        for c, chunk in enumerate(chunks):
-            bank = psum.tile([P, BANK], F32, name=f"bank{c}")
+        for start in range(0, places, CHUNK):
+            halves = (slice(start, start + HALF), slice(start + HALF, start + CHUNK))
+            banks = [psum.tile([P, HALF], F32, name="bank", tag="bank") for half in halves]
             for k in range(passes):
-                nc.tensor.matmul(bank[:], weights[:, k, :], chunk[:, k, :], start=(k == 0), stop=(k == passes - 1))
-            copy = nc.scalar.copy if c % 2 == 0 else nc.vector.tensor_copy
-            copy(table[:, c * BANK : (c + 1) * BANK], bank[:])
+                for bank, half in zip(banks, halves):
+                    nc.tensor.matmul(bank[:], weights[:, k, :], z_tile[:, k, half], start=(k == 0), stop=(k == passes - 1))
+            nc.scalar.copy(table[:, halves[0]], banks[0][:])
+            nc.vector.tensor_copy(table[:, halves[1]], banks[1][:])
 
-        columns = PIECE // GROUP
-        for u, stream in enumerate(streams):
-            summed = held.tile([P, PIECE], F32, name=f"summed{u}")
-            looked_up = table[:].indirect(offsets[:, u * columns : (u + 1) * columns])
-            nc.vector.tensor_tensor(summed[:], looked_up, stream[:], mybir.AluOpType.add)
-            nc.sync.dma_start(out[:, u * PIECE : (u + 1) * PIECE], summed[:])
+        summed = held.tile([P, entries], F32, name="summed")
+        for start in range(0, entries, PIECE):
+            piece = slice(start, start + PIECE)
+            looked_up = table[:].indirect(offsets[:, start // GROUP : (start + PIECE) // GROUP])
+            nc.vector.tensor_tensor(summed[:, piece], looked_up, stream[:, piece], mybir.AluOpType.add)
+            nc.sync.dma_start(out[:, piece], summed[:, piece])

@@ -1,8 +1,10 @@
+import itertools
+
 import concourse.mybir as mybir
 
 P = 128
-CHUNK = 512
-HALF = CHUNK // 2
+CHUNKS = (1024, 512, 512)
+STRIP = 256
 BANKS = 8
 PIECE = 512
 GROUP = 16
@@ -30,9 +32,10 @@ def tile_lookup_pjadd_out_kernel(tc, z, wt, base, offs, out):
         nc.scalar.dma_start(weights[:], wt_rows)
 
         z_tile = held.tile([P, passes, places], BF16, name="z_tile")
-        for start in range(0, places, CHUNK):
+        chunks = [slice(stop - width, stop) for width, stop in zip(CHUNKS, itertools.accumulate(CHUNKS))]
+        for chunk in chunks:
             for k in range(passes):
-                nc.sync.dma_start(z_tile[:, k, start : start + CHUNK], z_rows[:, k, start : start + CHUNK])
+                nc.sync.dma_start(z_tile[:, k, chunk], z_rows[:, k, chunk])
 
         offsets = held.tile([P, entries // GROUP], U16, name="offsets")
         nc.sync.dma_start(offsets[:], offs)
@@ -46,14 +49,15 @@ def tile_lookup_pjadd_out_kernel(tc, z, wt, base, offs, out):
         nc.tensor.matmul(unread[:], zeros[:], zeros[:].unsqueeze(1).to_broadcast([P, WARM, P]), start=True, stop=True)
 
         table = held.tile([P, places], F32, name="table")
-        for start in range(0, places, CHUNK):
-            halves = (slice(start, start + HALF), slice(start + HALF, start + CHUNK))
-            banks = [psum.tile([P, HALF], F32, name="bank", tag="bank") for half in halves]
+        for chunk in chunks:
+            strips = [slice(start, start + STRIP) for start in range(chunk.start, chunk.stop, STRIP)]
+            banks = [psum.tile([P, STRIP], F32, name="bank", tag="bank") for strip in strips]
             for k in range(passes):
-                for bank, half in zip(banks, halves):
-                    nc.tensor.matmul(bank[:], weights[:, k, :], z_tile[:, k, half], start=(k == 0), stop=(k == passes - 1))
-            nc.scalar.copy(table[:, halves[0]], banks[0][:])
-            nc.vector.tensor_copy(table[:, halves[1]], banks[1][:])
+                for bank, strip in zip(banks, strips):
+                    nc.tensor.matmul(bank[:], weights[:, k, :], z_tile[:, k, strip], start=(k == 0), stop=(k == passes - 1))
+            for s, (bank, strip) in enumerate(zip(banks, strips)):
+                copy = nc.scalar.copy if s % 2 == 0 else nc.vector.tensor_copy
+                copy(table[:, strip], bank[:])
 
         summed = held.tile([P, entries], F32, name="summed")
         for start in range(0, entries, PIECE):

@@ -5,6 +5,7 @@ import concourse.mybir as mybir
 P = 128
 CHUNKS = (1024, 512, 512)
 STRIP = 256
+LAST_STRIP = 128
 BANKS = 8
 PIECE = 512
 GROUP = 16
@@ -50,8 +51,9 @@ def tile_lookup_pjadd_out_kernel(tc, z, wt, base, offs, out):
 
         table = held.tile([P, places], F32, name="table")
         for chunk in chunks:
-            strips = [slice(start, start + STRIP) for start in range(chunk.start, chunk.stop, STRIP)]
-            banks = [psum.tile([P, STRIP], F32, name="bank", tag="bank") for strip in strips]
+            width = LAST_STRIP if chunk.stop == places else STRIP
+            strips = [slice(start, start + width) for start in range(chunk.start, chunk.stop, width)]
+            banks = [psum.tile([P, width], F32, name="bank", tag="bank") for strip in strips]
             for k in range(passes):
                 for bank, strip in zip(banks, strips):
                     nc.tensor.matmul(bank[:], weights[:, k, :], z_tile[:, k, strip], start=(k == 0), stop=(k == passes - 1))

import itertools

import concourse.mybir as mybir

P = 128
CHUNKS = (1024, 512, 512)
STRIP = 256
LAST_STRIP = 128
BANKS = 8
PIECE = 512
GROUP = 16
WARM = 3

FLOPS = 2 * 256 * 128 * 2048

BF16, F32, U16 = mybir.dt.bfloat16, mybir.dt.float32, mybir.dt.uint16


def tile_lookup_pjadd_out_kernel(tc, z, wt, base, offs, out):
    nc = tc.nc
    features, places = z.shape
    entries = base.shape[1]
    passes = features // P

    z_rows = z.rearrange("(p k) s -> p k s", k=passes)
    wt_rows = wt.rearrange("(p k) r -> p k r", k=passes)

    with (
        tc.tile_pool(name="held", bufs=1) as held,
        tc.psum_pool(name="psum", bufs=BANKS) as psum,
    ):
        weights = held.tile([P, passes, P], BF16, name="weights")
        nc.scalar.dma_start(weights[:], wt_rows)

        z_tile = held.tile([P, passes, places], BF16, name="z_tile")
        chunks = [slice(stop - width, stop) for width, stop in zip(CHUNKS, itertools.accumulate(CHUNKS))]
        for chunk in chunks:
            for k in range(passes):
                nc.sync.dma_start(z_tile[:, k, chunk], z_rows[:, k, chunk])

        offsets = held.tile([P, entries // GROUP], U16, name="offsets")
        nc.sync.dma_start(offsets[:], offs)
        stream = held.tile([P, entries], F32, name="stream")
        for start in range(0, entries, PIECE):
            nc.sync.dma_start(stream[:, start : start + PIECE], base[:, start : start + PIECE])

        zeros = held.tile([P, P], F32, name="zeros")
        nc.vector.memset(zeros[:], 0.0)
        unread = psum.tile([P, WARM, P], F32, name="unread", tag="bank")
        nc.tensor.matmul(unread[:], zeros[:], zeros[:].unsqueeze(1).to_broadcast([P, WARM, P]), start=True, stop=True)

        table = held.tile([P, places], F32, name="table")
        for chunk in chunks:
            width = LAST_STRIP if chunk.stop == places else STRIP
            strips = [slice(start, start + width) for start in range(chunk.start, chunk.stop, width)]
            banks = [psum.tile([P, width], F32, name="bank", tag="bank") for strip in strips]
            for k in range(passes):
                for bank, strip in zip(banks, strips):
                    nc.tensor.matmul(bank[:], weights[:, k, :], z_tile[:, k, strip], start=(k == 0), stop=(k == passes - 1))
            for s, (bank, strip) in enumerate(zip(banks, strips)):
                copy = nc.scalar.copy if s % 2 == 0 else nc.vector.tensor_copy
                copy(table[:, strip], bank[:])

        summed = held.tile([P, entries], F32, name="summed")
        for start in range(0, entries, PIECE):
            piece = slice(start, start + PIECE)
            looked_up = table[:].indirect(offsets[:, start // GROUP : (start + PIECE) // GROUP])
            nc.vector.tensor_tensor(summed[:, piece], looked_up, stream[:, piece], mybir.AluOpType.add)
            nc.sync.dma_start(out[:, piece], summed[:, piece])
